import numpy as np
CORES = [42,66,170,194,298,322,426,450,43]
N = 9
TK = 128
D = 128 * N
def setup_inputs(rng):
    return {"x": (rng.standard_normal((N, 128, TK), dtype=np.float32) + 2 * rng.standard_normal((N, 1, TK), dtype=np.float32))}
def reference(x):
    X = x.astype(np.float64).reshape(D, TK)
    m = X.sum(axis=0) / D
    Z = X - m
    c = Z.T @ Z / D
    return {"c": np.broadcast_to(c.astype(np.float32), (N, TK, TK)), "m": np.broadcast_to(m.astype(np.float32), (N, 1, TK))}

@@ -1,0 +1,125 @@
+from concourse.bass import DstId, RemoteDMATransfer
+from concourse.mybir import AluOpType
+
+W = 129
+PADW = 132
+
+SCRATCH = {
+    "xa": ("sbuf", [128, 128], "float32"),
+    "xb": ("sbuf", [128, PADW], "float32"),
+    "invd": ("sbuf", [128, PADW], "float32"),
+    "q": ("sbuf", [128, PADW], "float32"),
+    "l0": ("sbuf", [128, PADW], "float32"),
+    "l1": ("sbuf", [128, PADW], "float32"),
+    "l2": ("sbuf", [128, PADW], "float32"),
+    "l3": ("sbuf", [128, PADW], "float32"),
+    "l4": ("sbuf", [128, PADW], "float32"),
+    "r0": ("sbuf", [128, PADW], "float32"),
+    "lo": ("sbuf", [128, PADW], "float32"),
+    "p": ("sbuf", [128, PADW], "float32"),
+    "cf": ("sbuf", [128, PADW], "float32"),
+    "pw": ("psum", [128, 512], "float32"),
+    "pr": ("psum", [128, 512], "float32"),
+    "pm": ("psum", [128, 512], "float32"),
+}
+SEMAPHORES = ["ld", "ms", "vx", "mm", "qs", "a0", "a1", "a2", "a3", "a4", "ad", "rs", "rc", "b0", "b",
+              "ps", "t2", "c1", "c2", "st", "sent"]
+
+RACKS = ([42, 43, 66, 170, 194], [298, 322, 426, 450])
+PARTNER = {42: 426, 426: 42, 66: 450, 450: 66, 170: 298, 298: 170, 194: 322, 322: 194}
+EXTRA = 43
+OFF, ON = 0x00FF, 0xFF00
+
+
+def rank_program(g, core, T, topo):
+    if T.rank_of(core) is None:
+        return
+    S = T.sem
+    D = 128 * len(T.cores)
+    rack = RACKS[0] if core in RACKS[0] else RACKS[1]
+    me = rack.index(core)
+    v, te = g.vector, g.tensor
+
+    def did(d):
+        rid, pid = topo.addr(d, core)
+        return DstId(rid=rid, pnc=pid)
+
+    def same_chip(a, b):
+        return topo.host(a) == topo.host(b) and topo.chip(a) == topo.chip(b)
+
+    g.sync.dma_start(T.xa[:], T.x[:]).then_inc(S.ld, 16)
+    v.memset(T.xb[:, 0:4], 1.0).then_inc(S.ms, 1)
+    v.memset(T.invd[:, 0:W], 1.0 / D).then_inc(S.ms, 1)
+    v.wait_ge(S.ms, 2)
+    v.wait_ge(S.ld, 16)
+    v.tensor_copy(T.xb[:, 4:131], T.xa[:, 1:128]).then_inc(S.vx, 1)
+    te.wait_ge(S.ld, 16)
+    te.matmul(T.pw[:, 128:129], T.xa[:], T.xa[:, 0:1], True, True).then_inc(S.mm, 1)
+    te.wait_ge(S.ms, 2)
+    te.wait_ge(S.vx, 1)
+    te.matmul(T.pw[:, 0:128], T.xb[:, 3:131], T.xa[:], True, True).then_inc(S.mm, 1)
+    v.wait_ge(S.mm, 2)
+    v.tensor_tensor(T.q[:, 0:W], T.pw[:, 0:W], T.invd[:, 0:W], AluOpType.mult).then_inc(S.qs, 1)
+
+    sent = 0
+    g.wait_ge(S.qs, 1)
+    far = [d for d in rack if d != core and d != EXTRA and not same_chip(d, core)]
+    near = [d for d in rack if d != core and d != EXTRA and same_chip(d, core)]
+    slot = T["l%d" % me][:, 0:W]
+    trs = [RemoteDMATransfer(dst_ids=[did(d) for d in far], dma_engine_mask=OFF, remote_sem=S["a%d" % me],
+                             srcs=[T.q[:, 0:W]], dsts=[slot for d in far])]
+    sent += 8
+    if near:
+        trs.append(RemoteDMATransfer(dst_ids=[did(d) for d in near], dma_engine_mask=ON, remote_sem=S["a%d" % me],
+                                     srcs=[T.q[:, 0:W]], dsts=[slot for d in near]))
+        sent += 8
+    g.remote_dma_fused(trs, local_sem=S.sent)
+
+    if core != EXTRA:
+        def dist(s):
+            return 0 if same_chip(s, core) else (1 if topo.same_plane(s, core) else 2)
+        senders = sorted([s for s in rack if s != core], key=dist)
+        n = len(senders)
+        v.wait_ge(S.qs, 1)
+        for i, s in enumerate(senders):
+            k = rack.index(s)
+            v.wait_ge(S["a%d" % k], 8)
+            in0 = T.q[:, 0:W] if i == 0 else T.pr[:, 0:W]
+            if i > 0:
+                v.wait_ge(S.ad, i)
+            if i < n - 1:
+                v.tensor_tensor(T.pr[:, 0:W], in0, T["l%d" % k][:, 0:W], AluOpType.add).then_inc(S.ad, 1)
+            else:
+                v.tensor_tensor(T.r0[:, 0:W], in0, T["l%d" % k][:, 0:W], AluOpType.add).then_inc(S.rs, 1)
+        g.wait_ge(S.rs, 1)
+        dsts = [PARTNER[core]] + ([EXTRA] if PARTNER[core] == 42 else [])
+        trs = [RemoteDMATransfer(dst_ids=[did(d) for d in dsts], dma_engine_mask=OFF, remote_sem=S.b,
+                                 srcs=[T.r0[:, 0:W]], dsts=[T.lo[:, 0:W] for d in dsts])]
+        sent += 8
+        if core == 42:
+            trs.append(RemoteDMATransfer(dst_ids=[did(EXTRA)], dma_engine_mask=ON, remote_sem=S.b0,
+                                         srcs=[T.r0[:, 0:W]], dsts=[T.r0[:, 0:W]]))
+            sent += 8
+        g.remote_dma_fused(trs, local_sem=S.sent)
+        v.wait_ge(S.rs, 1)
+    else:
+        v.wait_ge(S.b0, 8)
+    v.tensor_copy(T.pr[:, 0:W], T.r0[:, 0:W]).then_inc(S.rc, 1)
+
+    v.wait_ge(S.rc, 1)
+    v.wait_ge(S.b, 8)
+    v.tensor_tensor(T.p[:, 0:W], T.pr[:, 0:W], T.lo[:, 0:W], AluOpType.add).then_inc(S.ps, 1)
+    te.wait_ge(S.ps, 1)
+    te.matmul(T.pm[:, 0:128], T.p[0:1, 0:128], T.p[0:1, 0:128], True, True).then_inc(S.t2, 1)
+    g.scalar.wait_ge(S.ps, 1)
+    g.scalar.dma_start(T.m[:], T.p[0:1, 0:128]).then_inc(S.st, 16)
+    v.wait_ge(S.ps, 1)
+    v.wait_ge(S.t2, 1)
+    v.tensor_tensor(T.cf[:, 0:128], T.p[:, 0:128], T.pm[:, 0:128], AluOpType.subtract).then_inc(S.c1, 1)
+    v.tensor_tensor(T.cf[:, 128:129], T.p[:, 128:129], T.pm[:, 0:1], AluOpType.subtract).then_inc(S.c2, 1)
+    g.sync.wait_ge(S.c1, 1)
+    g.sync.dma_start(T.c[1:128, :], T.cf[1:128, 0:128]).then_inc(S.st, 16)
+    g.scalar.wait_ge(S.c2, 1)
+    g.scalar.dma_start(T.c[0:1, :], T.cf[:, 128:129]).then_inc(S.st, 16)
+    g.wait_ge(S.st, 48)
+    g.wait_ge(S.sent, sent)

@@ -3,30 +3,36 @@ from concourse.mybir import AluOpType
 
 W = 129
 PADW = 132
+WP = 65
+PADP = 68
+PC = ((0, 65), (64, 129))
 
 SCRATCH = {
     "xa": ("sbuf", [128, 128], "float32"),
     "xb": ("sbuf", [128, PADW], "float32"),
     "invd": ("sbuf", [128, PADW], "float32"),
     "q": ("sbuf", [128, PADW], "float32"),
-    "l0": ("sbuf", [128, PADW], "float32"),
-    "l1": ("sbuf", [128, PADW], "float32"),
-    "l2": ("sbuf", [128, PADW], "float32"),
-    "l3": ("sbuf", [128, PADW], "float32"),
-    "l4": ("sbuf", [128, PADW], "float32"),
-    "r0": ("sbuf", [128, PADW], "float32"),
-    "lo": ("sbuf", [128, PADW], "float32"),
+    "l0": ("sbuf", [128, PADP], "float32"),
+    "l1": ("sbuf", [128, PADP], "float32"),
+    "l2": ("sbuf", [128, PADP], "float32"),
+    "l3": ("sbuf", [128, PADP], "float32"),
+    "l4": ("sbuf", [128, PADP], "float32"),
+    "z00": ("sbuf", [128, PADP], "float32"),
+    "z01": ("sbuf", [128, PADP], "float32"),
+    "z10": ("sbuf", [128, PADP], "float32"),
+    "z11": ("sbuf", [128, PADP], "float32"),
     "p": ("sbuf", [128, PADW], "float32"),
     "cf": ("sbuf", [128, PADW], "float32"),
     "pw": ("psum", [128, 512], "float32"),
+    "pa": ("psum", [128, 512], "float32"),
     "pr": ("psum", [128, 512], "float32"),
     "pm": ("psum", [128, 512], "float32"),
 }
-SEMAPHORES = ["ld", "ms", "vx", "mm", "qs", "a0", "a1", "a2", "a3", "a4", "ad", "rs", "rc", "b0", "b",
-              "ps", "t2", "c1", "c2", "st", "sent"]
+SEMAPHORES = ["ld", "ms", "vx", "mm", "qs", "a0", "a1", "a2", "a3", "a4", "ad", "rs", "rc",
+              "s00", "s01", "s10", "s11", "ps", "t2", "c1", "c2", "st", "sent"]
 
 RACKS = ([42, 43, 66, 170, 194], [298, 322, 426, 450])
-PARTNER = {42: 426, 426: 42, 66: 450, 450: 66, 170: 298, 298: 170, 194: 322, 322: 194}
+CABLED = {0: 3, 3: 0, 1: 2, 2: 1}
 EXTRA = 43
 OFF, ON = 0x00FF, 0xFF00
 
@@ -36,7 +42,8 @@ def rank_program(g, core, T, topo):
         return
     S = T.sem
     D = 128 * len(T.cores)
-    rack = RACKS[0] if core in RACKS[0] else RACKS[1]
+    rk = 0 if core in RACKS[0] else 1
+    rack = RACKS[rk]
     me = rack.index(core)
     v, te = g.vector, g.tensor
 
@@ -46,6 +53,9 @@ def rank_program(g, core, T, topo):
 
     def same_chip(a, b):
         return topo.host(a) == topo.host(b) and topo.chip(a) == topo.chip(b)
+
+    def piece(d):
+        return 0 if topo.chip(d) == 5 else 1
 
     g.sync.dma_start(T.xa[:], T.x[:]).then_inc(S.ld, 16)
     v.memset(T.xb[:, 0:4], 1.0).then_inc(S.ms, 1)
@@ -63,19 +73,27 @@ def rank_program(g, core, T, topo):
 
     sent = 0
     g.wait_ge(S.qs, 1)
-    far = [d for d in rack if d != core and d != EXTRA and not same_chip(d, core)]
-    near = [d for d in rack if d != core and d != EXTRA and same_chip(d, core)]
-    slot = T["l%d" % me][:, 0:W]
-    trs = [RemoteDMATransfer(dst_ids=[did(d) for d in far], dma_engine_mask=OFF, remote_sem=S["a%d" % me],
-                             srcs=[T.q[:, 0:W]], dsts=[slot for d in far])]
-    sent += 8
-    if near:
-        trs.append(RemoteDMATransfer(dst_ids=[did(d) for d in near], dma_engine_mask=ON, remote_sem=S["a%d" % me],
-                                     srcs=[T.q[:, 0:W]], dsts=[slot for d in near]))
-        sent += 8
+    slot = T["l%d" % me][:, 0:WP]
+    trs = []
+    for j in (0, 1):
+        src = T.q[:, PC[j][0]:PC[j][1]]
+        red = [d for d in rack if d != core and d != EXTRA and piece(d) == j]
+        far = [d for d in red if not same_chip(d, core)]
+        near = [d for d in red if same_chip(d, core)]
+        if far:
+            trs.append(RemoteDMATransfer(dst_ids=[did(d) for d in far], dma_engine_mask=0x0F << (4 * j),
+                                         remote_sem=S["a%d" % me], srcs=[src], dsts=[slot for d in far]))
+            sent += 4
+        if near:
+            trs.append(RemoteDMATransfer(dst_ids=[did(d) for d in near], dma_engine_mask=ON,
+                                         remote_sem=S["a%d" % me], srcs=[src], dsts=[slot for d in near]))
+            sent += 8
     g.remote_dma_fused(trs, local_sem=S.sent)
 
     if core != EXTRA:
+        mj = piece(core)
+        zown = T["z%d%d" % (rk, mj)][:, 0:WP]
+
         def dist(s):
             return 0 if same_chip(s, core) else (1 if topo.same_plane(s, core) else 2)
         senders = sorted([s for s in rack if s != core], key=dist)
@@ -83,37 +101,49 @@ def rank_program(g, core, T, topo):
         v.wait_ge(S.qs, 1)
         for i, s in enumerate(senders):
             k = rack.index(s)
-            v.wait_ge(S["a%d" % k], 8)
-            in0 = T.q[:, 0:W] if i == 0 else T.pr[:, 0:W]
+            v.wait_ge(S["a%d" % k], 8 if same_chip(s, core) else 4)
+            in0 = T.q[:, PC[mj][0]:PC[mj][1]] if i == 0 else T.pa[:, 0:WP]
             if i > 0:
                 v.wait_ge(S.ad, i)
             if i < n - 1:
-                v.tensor_tensor(T.pr[:, 0:W], in0, T["l%d" % k][:, 0:W], AluOpType.add).then_inc(S.ad, 1)
+                v.tensor_tensor(T.pa[:, 0:WP], in0, T["l%d" % k][:, 0:WP], AluOpType.add).then_inc(S.ad, 1)
             else:
-                v.tensor_tensor(T.r0[:, 0:W], in0, T["l%d" % k][:, 0:W], AluOpType.add).then_inc(S.rs, 1)
+                v.tensor_tensor(zown, in0, T["l%d" % k][:, 0:WP], AluOpType.add).then_inc(S.rs, 1)
         g.wait_ge(S.rs, 1)
-        dsts = [PARTNER[core]] + ([EXTRA] if PARTNER[core] == 42 else [])
-        trs = [RemoteDMATransfer(dst_ids=[did(d) for d in dsts], dma_engine_mask=OFF, remote_sem=S.b,
-                                 srcs=[T.r0[:, 0:W]], dsts=[T.lo[:, 0:W] for d in dsts])]
+        hs = (topo.host(core), CABLED[topo.host(core)])
+        dsts = [d for d in T.cores if d != core and topo.host(d) in hs]
+        far = [d for d in dsts if not same_chip(d, core)]
+        near = [d for d in dsts if same_chip(d, core)]
+        trs = [RemoteDMATransfer(dst_ids=[did(d) for d in far], dma_engine_mask=OFF, remote_sem=S["s%d%d" % (rk, mj)],
+                                 srcs=[zown], dsts=[zown for d in far])]
         sent += 8
-        if core == 42:
-            trs.append(RemoteDMATransfer(dst_ids=[did(EXTRA)], dma_engine_mask=ON, remote_sem=S.b0,
-                                         srcs=[T.r0[:, 0:W]], dsts=[T.r0[:, 0:W]]))
+        if near:
+            trs.append(RemoteDMATransfer(dst_ids=[did(d) for d in near], dma_engine_mask=ON,
+                                         remote_sem=S["s%d%d" % (rk, mj)], srcs=[zown], dsts=[zown for d in near]))
             sent += 8
         g.remote_dma_fused(trs, local_sem=S.sent)
-        v.wait_ge(S.rs, 1)
     else:
-        v.wait_ge(S.b0, 8)
-    v.tensor_copy(T.pr[:, 0:W], T.r0[:, 0:W]).then_inc(S.rc, 1)
+        mj = None
 
-    v.wait_ge(S.rc, 1)
-    v.wait_ge(S.b, 8)
-    v.tensor_tensor(T.p[:, 0:W], T.pr[:, 0:W], T.lo[:, 0:W], AluOpType.add).then_inc(S.ps, 1)
-    te.wait_ge(S.ps, 1)
+    OUT = ((0, 64), (64, 129))
+    first = 0 if mj is None else mj
+    for j in (first, 1 - first):
+        if j == mj:
+            v.wait_ge(S.rs, 1)
+        else:
+            v.wait_ge(S["s%d%d" % (rk, j)], 8)
+        a, b = OUT[j]
+        v.tensor_copy(T.pr[:, a:b], T["z%d%d" % (rk, j)][:, 0:b - a]).then_inc(S.rc, 1)
+    v.wait_ge(S.rc, 2)
+    for j in (first, 1 - first):
+        v.wait_ge(S["s%d%d" % (1 - rk, j)], 8)
+        a, b = OUT[j]
+        v.tensor_tensor(T.p[:, a:b], T.pr[:, a:b], T["z%d%d" % (1 - rk, j)][:, 0:b - a], AluOpType.add).then_inc(S.ps, 1)
+    te.wait_ge(S.ps, 2)
     te.matmul(T.pm[:, 0:128], T.p[0:1, 0:128], T.p[0:1, 0:128], True, True).then_inc(S.t2, 1)
-    g.scalar.wait_ge(S.ps, 1)
+    g.scalar.wait_ge(S.ps, 2)
     g.scalar.dma_start(T.m[:], T.p[0:1, 0:128]).then_inc(S.st, 16)
-    v.wait_ge(S.ps, 1)
+    v.wait_ge(S.ps, 2)
     v.wait_ge(S.t2, 1)
     v.tensor_tensor(T.cf[:, 0:128], T.p[:, 0:128], T.pm[:, 0:128], AluOpType.subtract).then_inc(S.c1, 1)
     v.tensor_tensor(T.cf[:, 128:129], T.p[:, 128:129], T.pm[:, 0:1], AluOpType.subtract).then_inc(S.c2, 1)

from concourse.bass import DstId, RemoteDMATransfer
from concourse.mybir import AluOpType

W = 129
PADW = 132
WP = 65
PADP = 68
PC = ((0, 65), (64, 129))

SCRATCH = {
    "xa": ("sbuf", [128, 128], "float32"),
    "xb": ("sbuf", [128, PADW], "float32"),
    "invd": ("sbuf", [128, PADW], "float32"),
    "q": ("sbuf", [128, PADW], "float32"),
    "l0": ("sbuf", [128, PADP], "float32"),
    "l1": ("sbuf", [128, PADP], "float32"),
    "l2": ("sbuf", [128, PADP], "float32"),
    "l3": ("sbuf", [128, PADP], "float32"),
    "l4": ("sbuf", [128, PADP], "float32"),
    "z00": ("sbuf", [128, PADP], "float32"),
    "z01": ("sbuf", [128, PADP], "float32"),
    "z10": ("sbuf", [128, PADP], "float32"),
    "z11": ("sbuf", [128, PADP], "float32"),
    "p": ("sbuf", [128, PADW], "float32"),
    "cf": ("sbuf", [128, PADW], "float32"),
    "pw": ("psum", [128, 512], "float32"),
    "pa": ("psum", [128, 512], "float32"),
    "pr": ("psum", [128, 512], "float32"),
    "pm": ("psum", [128, 512], "float32"),
}
SEMAPHORES = ["ld", "ms", "vx", "mm", "qs", "a0", "a1", "a2", "a3", "a4", "ad", "rs", "rc",
              "s00", "s01", "s10", "s11", "ps", "t2", "c1", "c2", "st", "sent"]

RACKS = ([42, 43, 66, 170, 194], [298, 322, 426, 450])
CABLED = {0: 3, 3: 0, 1: 2, 2: 1}
EXTRA = 43
OFF, ON = 0x00FF, 0xFF00


def rank_program(g, core, T, topo):
    if T.rank_of(core) is None:
        return
    S = T.sem
    D = 128 * len(T.cores)
    rk = 0 if core in RACKS[0] else 1
    rack = RACKS[rk]
    me = rack.index(core)
    v, te = g.vector, g.tensor

    def did(d):
        rid, pid = topo.addr(d, core)
        return DstId(rid=rid, pnc=pid)

    def same_chip(a, b):
        return topo.host(a) == topo.host(b) and topo.chip(a) == topo.chip(b)

    def piece(d):
        return 0 if topo.chip(d) == 5 else 1

    g.sync.dma_start(T.xa[:], T.x[:]).then_inc(S.ld, 16)
    v.memset(T.xb[:, 0:4], 1.0).then_inc(S.ms, 1)
    v.memset(T.invd[:, 0:W], 1.0 / D).then_inc(S.ms, 1)
    v.wait_ge(S.ms, 2)
    v.wait_ge(S.ld, 16)
    v.tensor_copy(T.xb[:, 4:131], T.xa[:, 1:128]).then_inc(S.vx, 1)
    te.wait_ge(S.ld, 16)
    te.matmul(T.pw[:, 128:129], T.xa[:], T.xa[:, 0:1], True, True).then_inc(S.mm, 1)
    te.wait_ge(S.ms, 2)
    te.wait_ge(S.vx, 1)
    te.matmul(T.pw[:, 0:128], T.xb[:, 3:131], T.xa[:], True, True).then_inc(S.mm, 1)
    v.wait_ge(S.mm, 2)
    v.tensor_tensor(T.q[:, 0:W], T.pw[:, 0:W], T.invd[:, 0:W], AluOpType.mult).then_inc(S.qs, 1)

    sent = 0
    g.wait_ge(S.qs, 1)
    slot = T["l%d" % me][:, 0:WP]
    trs = []
    for j in (0, 1):
        src = T.q[:, PC[j][0]:PC[j][1]]
        red = [d for d in rack if d != core and d != EXTRA and piece(d) == j]
        far = [d for d in red if not same_chip(d, core)]
        near = [d for d in red if same_chip(d, core)]
        if far:
            trs.append(RemoteDMATransfer(dst_ids=[did(d) for d in far], dma_engine_mask=0x0F << (4 * j),
                                         remote_sem=S["a%d" % me], srcs=[src], dsts=[slot for d in far]))
            sent += 4
        if near:
            trs.append(RemoteDMATransfer(dst_ids=[did(d) for d in near], dma_engine_mask=ON,
                                         remote_sem=S["a%d" % me], srcs=[src], dsts=[slot for d in near]))
            sent += 8
    g.remote_dma_fused(trs, local_sem=S.sent)

    if core != EXTRA:
        mj = piece(core)
        zown = T["z%d%d" % (rk, mj)][:, 0:WP]

        def dist(s):
            return 0 if same_chip(s, core) else (1 if topo.same_plane(s, core) else 2)
        senders = sorted([s for s in rack if s != core], key=dist)
        n = len(senders)
        v.wait_ge(S.qs, 1)
        for i, s in enumerate(senders):
            k = rack.index(s)
            v.wait_ge(S["a%d" % k], 8 if same_chip(s, core) else 4)
            in0 = T.q[:, PC[mj][0]:PC[mj][1]] if i == 0 else T.pa[:, 0:WP]
            if i > 0:
                v.wait_ge(S.ad, i)
            if i < n - 1:
                v.tensor_tensor(T.pa[:, 0:WP], in0, T["l%d" % k][:, 0:WP], AluOpType.add).then_inc(S.ad, 1)
            else:
                v.tensor_tensor(zown, in0, T["l%d" % k][:, 0:WP], AluOpType.add).then_inc(S.rs, 1)
        g.wait_ge(S.rs, 1)
        hs = (topo.host(core), CABLED[topo.host(core)])
        dsts = [d for d in T.cores if d != core and topo.host(d) in hs]
        far = [d for d in dsts if not same_chip(d, core)]
        near = [d for d in dsts if same_chip(d, core)]
        trs = [RemoteDMATransfer(dst_ids=[did(d) for d in far], dma_engine_mask=OFF, remote_sem=S["s%d%d" % (rk, mj)],
                                 srcs=[zown], dsts=[zown for d in far])]
        sent += 8
        if near:
            trs.append(RemoteDMATransfer(dst_ids=[did(d) for d in near], dma_engine_mask=ON,
                                         remote_sem=S["s%d%d" % (rk, mj)], srcs=[zown], dsts=[zown for d in near]))
            sent += 8
        g.remote_dma_fused(trs, local_sem=S.sent)
    else:
        mj = None

    OUT = ((0, 64), (64, 129))
    first = 0 if mj is None else mj
    for j in (first, 1 - first):
        if j == mj:
            v.wait_ge(S.rs, 1)
        else:
            v.wait_ge(S["s%d%d" % (rk, j)], 8)
        a, b = OUT[j]
        v.tensor_copy(T.pr[:, a:b], T["z%d%d" % (rk, j)][:, 0:b - a]).then_inc(S.rc, 1)
    v.wait_ge(S.rc, 2)
    for j in (first, 1 - first):
        v.wait_ge(S["s%d%d" % (1 - rk, j)], 8)
        a, b = OUT[j]
        v.tensor_tensor(T.p[:, a:b], T.pr[:, a:b], T["z%d%d" % (1 - rk, j)][:, 0:b - a], AluOpType.add).then_inc(S.ps, 1)
    te.wait_ge(S.ps, 2)
    te.matmul(T.pm[:, 0:128], T.p[0:1, 0:128], T.p[0:1, 0:128], True, True).then_inc(S.t2, 1)
    g.scalar.wait_ge(S.ps, 2)
    g.scalar.dma_start(T.m[:], T.p[0:1, 0:128]).then_inc(S.st, 16)
    v.wait_ge(S.ps, 2)
    v.wait_ge(S.t2, 1)
    v.tensor_tensor(T.cf[:, 0:128], T.p[:, 0:128], T.pm[:, 0:128], AluOpType.subtract).then_inc(S.c1, 1)
    v.tensor_tensor(T.cf[:, 128:129], T.p[:, 128:129], T.pm[:, 0:1], AluOpType.subtract).then_inc(S.c2, 1)
    g.sync.wait_ge(S.c1, 1)
    g.sync.dma_start(T.c[1:128, :], T.cf[1:128, 0:128]).then_inc(S.st, 16)
    g.scalar.wait_ge(S.c2, 1)
    g.scalar.dma_start(T.c[0:1, :], T.cf[:, 128:129]).then_inc(S.st, 16)
    g.wait_ge(S.st, 48)
    g.wait_ge(S.sent, sent)
